import numpy as np
import ml_dtypes


def mxq(x, axis, fmt="e4m3"):
    dtype, down = {"e4m3": (ml_dtypes.float8_e4m3fn, 7), "e5m2": (ml_dtypes.float8_e5m2, 14)}[fmt]
    v = np.moveaxis(np.asarray(x, np.float32).astype(ml_dtypes.bfloat16).astype(np.float64), axis, -1)
    blocks = v.reshape(v.shape[:-1] + (-1, 32))
    amax = np.abs(blocks).max(-1, keepdims=True)
    byte = np.maximum(np.where(amax > 0, np.frexp(amax)[1] - 1 + 127, 0) - down, 1)
    scale = np.exp2(byte - 127.0)
    codes = (blocks / scale).astype(np.float32).astype(dtype).astype(np.float64)
    return np.moveaxis((codes * scale).reshape(v.shape), -1, axis)


WIDE = False


def mx_kscale(k):
    if not WIDE:
        return np.ones(k)
    levels = np.array([10, -10, 5, -5, 0])
    if k % 512:
        return np.exp2(np.random.permutation(np.resize(levels, k // 32))).repeat(32)
    a = np.empty((k // 512, 16))
    for p in range(k // 512):
        a[p, :8] = np.random.permutation(np.resize(levels, 8))
        for g in range(8):
            far = levels[np.abs(levels - a[p, g]) >= 10]
            a[p, g + 8] = far[np.random.randint(len(far))]
    return np.exp2(a.ravel()).repeat(32)


def f64(x):
    return np.asarray(x).astype(np.float64)


def striped(idx):
    return np.tile(idx.reshape(-1, 16).T, (8, 1)).astype(np.uint16)


def unstriped(offs):
    return offs[:16].T.reshape(-1).astype(np.int64)


def striped8(idx):
    return np.concatenate([x.reshape(-1, 16).T for x in idx]).astype(np.uint16)


def runs(offs, k):
    lists = np.stack([offs[16 * r : 16 * r + 16].T.reshape(-1) for r in range(8)]).astype(np.int64)
    return lists[np.arange(k) % 512 // 64]


def pack_weight(w):
    k, n = w.shape
    w = f64(np.asarray(w, np.float32).astype(ml_dtypes.bfloat16)).reshape(k // 32, 32, n)
    amax = np.abs(w).max(1)
    byte = np.clip(np.where(amax > 0, np.frexp(amax)[1] - 1 + 127 - 7, 1), 1, 254)
    scaled = (w * np.exp2(127.0 - byte)[:, None, :]).reshape(k, n).astype(np.float32)
    words = np.ascontiguousarray(scaled.reshape(k // 512, 128, 4, n).transpose(0, 1, 3, 2)).astype(ml_dtypes.float8_e4m3fn).view(np.uint8)
    return words, np.ascontiguousarray(byte.astype(np.uint8).reshape(k // 512, 16, n))


def unpack_weight(words, scales):
    g, p, n, _ = words.shape
    vals = np.ascontiguousarray(words).view(ml_dtypes.float8_e4m3fn).astype(np.float64) * np.repeat(np.exp2(scales.astype(np.float64) - 127.0), 8, axis=1)[..., None]
    return vals.transpose(0, 1, 3, 2).reshape(g * 512, n)


E2M1 = np.array([0.0, 0.5, 1.0, 1.5, 2.0, 3.0, 4.0, 6.0, -0.0, -0.5, -1.0, -1.5, -2.0, -3.0, -4.0, -6.0])


def pack_fp4(w):
    k, n = w.shape
    w = f64(np.asarray(w, np.float32).astype(ml_dtypes.bfloat16)).reshape(k // 32, 32, n)
    amax = np.abs(w).max(1)
    mant, ex = np.frexp(amax / 6.0)
    byte = np.clip(np.where(amax > 0, np.where(mant > 0.5, ex, ex - 1) + 127, 1), 1, 254)
    scaled = (w * np.exp2(127.0 - byte)[:, None, :]).reshape(k, n).astype(np.float32)
    c = np.ascontiguousarray(scaled.reshape(k // 512, 128, 4, n).transpose(0, 1, 3, 2)).astype(ml_dtypes.float4_e2m1fn).view(np.uint8) & 0xF
    words = (c[..., 0::2] | (c[..., 1::2] << 4)).reshape(k // 512, 128, 2 * n)
    return np.ascontiguousarray(words), np.ascontiguousarray(byte.astype(np.uint8).reshape(k // 512, 16, n))


def unpack_fp4(words, scales):
    g, _, n = scales.shape
    words = np.ascontiguousarray(words).reshape(g, 128, n, 2)
    nib = np.empty((g, 128, n, 4), np.uint8)
    nib[..., 0::2] = words & 0xF
    nib[..., 1::2] = words >> 4
    vals = E2M1[nib] * np.repeat(np.exp2(scales.astype(np.float64) - 127.0), 8, axis=1)[..., None]
    return vals.transpose(0, 1, 3, 2).reshape(g * 512, n)


def sigmoid(v):
    return 1.0 / (1.0 + np.exp(-np.maximum(v, -700.0)))

def planes(y):
    n, m = y.shape
    v = y.astype(np.float32).astype(ml_dtypes.bfloat16).astype(np.float64).reshape(n // 32, 32, m)
    top = np.abs(v).max(1)
    byte = np.clip(np.where(top > 0, np.frexp(top)[1] - 1 + 127 - 7, 1), 1, 254)
    codes = (v * np.exp2(127.0 - byte)[:, None, :]).reshape(n, m).astype(np.float32).astype(ml_dtypes.float8_e4m3fn).view(np.uint8)
    words = codes.reshape(n // 512, 128, 4, m).transpose(0, 1, 3, 2)
    return np.ascontiguousarray(words), np.ascontiguousarray(byte.astype(np.uint8).reshape(n // 512, 16, m))


K, T, S, H, G = 512, 1024, 512, 512, 2048


def setup_inputs():
    n = np.random.standard_normal
    s = mx_kscale(K)[:, None]
    packed_xT = pack_weight(n((K, T)) * s)
    packed_w1 = pack_fp4(n((K, H)) / np.sqrt(K) / s)
    packed_w2 = pack_fp4(n((K, H)) / np.sqrt(K) / s)
    packed_dT = pack_weight(n((K, G)) / s)
    return {
        "x_words": packed_xT[0],
        "x_scales": packed_xT[1],
        "w1_words": packed_w1[0],
        "w1_scales": packed_w1[1],
        "w2_words": packed_w2[0],
        "w2_scales": packed_w2[1],
        "gs": (np.random.uniform(0.5, 1.5, (K, 1)) * s).astype(np.float32),
        "d_words": packed_dT[0],
        "d_scales": packed_dT[1],
        "offs": striped(np.random.permutation(T)[:S]),
        "two": striped(np.random.permutation(T)[:S]),
        "n1": striped8(np.stack([np.random.permutation(S) for _ in range(8)])),
        "n2": striped8(np.stack([np.random.permutation(S) for _ in range(8)])),
        "k1": striped8(np.random.randint(0, G, (8, H))),
        "n3": striped8(np.stack([np.random.permutation(S) for _ in range(8)])),
        "n4": striped8(np.stack([np.random.permutation(S) for _ in range(8)])),
    }


def reference(x_words, x_scales, w1_words, w1_scales, w2_words, w2_scales, gs, d_words, d_scales, offs, two, n1, n2, k1, n3, n4):
    d_k1 = unpack_weight(d_words, d_scales)[np.arange(K)[:, None], runs(k1, K)]
    xq = unpack_weight(x_words, x_scales)[:, unstriped(offs)]
    y = unpack_fp4(w1_words, w1_scales).T @ xq
    x_two = unpack_weight(x_words, x_scales)[:, unstriped(two)]
    d = unpack_fp4(w2_words, w2_scales).T @ x_two
    z = f64(gs) * (y + (sigmoid(d[np.arange(H)[:, None], runs(n2, H)] - d)) * (y[np.arange(H)[:, None], runs(n1, H)] - y))
    h = 0.0625 * ((d_k1.T @ mxq(z, 0, "e4m3")))
    out_0 = (h[np.arange(H)[:, None], runs(n3, H)]) * (h[np.arange(H)[:, None], runs(n4, H)])
    return (out_0,) + planes(out_0)

@@ -1,0 +1,205 @@
+from contextlib import ExitStack
+
+import concourse.mybir as mybir
+
+F32 = mybir.dt.float32
+BF16 = mybir.dt.bfloat16
+I32 = mybir.dt.int32
+U32 = mybir.dt.uint32
+U16 = mybir.dt.uint16
+U8 = mybir.dt.uint8
+FP8X4 = mybir.dt.float8_e4m3fn_x4
+FP4X4 = mybir.dt.float4_e2m1fn_x4
+ACT = mybir.ActivationFunctionType
+ALU = mybir.AluOpType
+
+P = 128
+PACK = 4
+K = 512
+T = 1024
+S = 512
+G = 2048
+FLOPS = 3 * 2 * K * K * S
+HALF = S // 2
+
+
+def tile_picked_twqpullbprod_none_po_kernel(
+    tc, x_words, x_scales, w1_words, w1_scales, w2_words, w2_scales, gs, d_words, d_scales,
+    offs, two, n1, n2, k1, n3, n4, out_0, out_1, out_2,
+):
+    nc = tc.nc
+    with ExitStack() as ctx:
+        keep = ctx.enter_context(tc.tile_pool(name="keep", bufs=1))
+        psum = ctx.enter_context(tc.psum_pool(name="psum", bufs=1))
+
+        def sb(name, shape, dtype):
+            return keep.tile(shape, dtype, name=name, align_bytes=64)
+
+        def load_list(name, src):
+            tile = sb(name, [P, S // 16], U16)
+            nc.sync.dma_start(tile[:], src)
+            return tile
+
+        def entries(lst, cols):
+            return lst[:, cols.start // 16 : cols.stop // 16]
+
+        def load_scale_rows(queue, plane, src):
+            for q in range(4):
+                queue.dma_start(plane[32 * q : 32 * q + 4, :].bitcast(I32), src[0, 4 * q : 4 * q + 4, :].bitcast(I32))
+
+        def zeroed(engine, name, width):
+            plane = sb(name, [P, width], U8)
+            engine.memset(plane[:].bitcast(I32), 0)
+            return plane
+
+        warm = sb("warm", [P, 2], F32)
+        nc.vector.memset(warm[:, 0:1], 0.0)
+        nc.scalar.activation(warm[:, 1:2], warm[:, 0:1], ACT.Sigmoid)
+
+        w2_sc_raw = zeroed(nc.vector, "w2_sc_raw", K)
+        x_sc = zeroed(nc.vector, "x_sc", T)
+        w1_sc_raw = zeroed(nc.vector, "w1_sc_raw", K)
+        d_sc = zeroed(nc.gpsimd, "d_sc", G)
+        dk_sc = zeroed(nc.gpsimd, "dk_sc", K)
+
+        x_w = sb("x_w", [P, T], I32)
+        nc.sync.dma_start(x_w[:], x_words[0].rearrange("p n t -> p (n t)").bitcast(I32))
+        two_l = load_list("two_l", two)
+        w2_raw = sb("w2_raw", [P, 2 * K], U8)
+        nc.sync.dma_start(w2_raw[:].bitcast(I32), w2_words[0].bitcast(I32))
+        w1_raw = sb("w1_raw", [P, 2 * K], U8)
+        nc.sync.dma_start(w1_raw[:].bitcast(I32), w1_words[0].bitcast(I32))
+        load_scale_rows(nc.scalar, w2_sc_raw, w2_scales)
+        load_scale_rows(nc.sync, x_sc, x_scales)
+        offs_l = load_list("offs_l", offs)
+        load_scale_rows(nc.scalar, w1_sc_raw, w1_scales)
+        n2_l = load_list("n2_l", n2)
+        k1_l = load_list("k1_l", k1)
+        d_w = sb("d_w", [P, G], I32)
+        nc.sync.dma_start(d_w[:], d_words[0].rearrange("p n t -> p (n t)").bitcast(I32))
+        nc.sync.dma_start(d_sc[0:P:8, :].bitcast(I32), d_scales[0].bitcast(I32))
+        gs_sb = sb("gs_sb", [P, PACK], F32)
+        nc.sync.dma_start(gs_sb[:], gs.rearrange("(p t) o -> p (t o)", t=PACK))
+        n1_l = load_list("n1_l", n1)
+        n3_l = load_list("n3_l", n3)
+        n4_l = load_list("n4_l", n4)
+
+        def deal_fp4(name, raw):
+            dealt = sb(name, [P, PACK, P, 2], U8)
+            nc.vector.tensor_copy(dealt[:], raw[:].rearrange("p (m t b) -> p t m b", t=PACK, b=2))
+            return dealt
+
+        def deal(name, raw, dtype):
+            dealt = sb(name, [P, PACK, P], dtype)
+            nc.vector.tensor_copy(dealt[:], raw[:].rearrange("p (m t) -> p t m", t=PACK))
+            return dealt
+
+        def pick(name, window, lst, dtype):
+            picked = sb(name, [P, S], dtype)
+            nc.vector.tensor_copy(picked[:], window.indirect(lst[:]))
+            return picked
+
+        banks = [psum.tile([P, S], F32, name="bank%d" % b) for b in range(8)]
+
+        def project(first_bank, w, w_sc, xw, xs):
+            for t in range(PACK):
+                nc.tensor.matmul_mx(
+                    out=banks[first_bank + t][:],
+                    lhsT=w[:, t].rearrange("p m b -> p (m b)").bitcast(FP4X4), lhsT_scale=w_sc[:, t, :],
+                    rhs=xw[:].bitcast(FP8X4), rhs_scale=xs[:], start=True, stop=True,
+                )
+
+        w2 = deal_fp4("w2", w2_raw)
+        w1 = deal_fp4("w1", w1_raw)
+        w2_sc = deal("w2_sc", w2_sc_raw, U8)
+        x2_w = pick("x2_w", x_w[:].bitcast(U32), two_l, U32)
+        x2_sc = pick("x2_sc", x_sc[:], two_l, U8)
+        project(0, w2, w2_sc, x2_w, x2_sc)
+        x1_w = pick("x1_w", x_w[:].bitcast(U32), offs_l, U32)
+        x1_sc = pick("x1_sc", x_sc[:], offs_l, U8)
+        w1_sc = deal("w1_sc", w1_sc_raw, U8)
+        project(PACK, w1, w1_sc, x1_w, x1_sc)
+
+        d_win = [sb("d_win%d" % t, [P, S], F32) for t in range(PACK)]
+        d_own = [sb("d_own%d" % t, [P, S], F32) for t in range(PACK)]
+        for t in range(PACK):
+            nc.scalar.copy(d_win[t][:], banks[t][:])
+            nc.scalar.copy(d_own[t][:], banks[t][:])
+        y_win = [sb("y_win%d" % t, [P, S], F32) for t in range(PACK)]
+        y_own = sb("y_own", [P, PACK, S], F32)
+        for t in range(PACK):
+            nc.scalar.activation(y_win[t][:], banks[PACK + t][:], ACT.Copy, scale=gs_sb[:, t : t + 1])
+            nc.scalar.activation(y_own[:, t, :], banks[PACK + t][:], ACT.Copy, scale=gs_sb[:, t : t + 1])
+
+        dk_sc_picked = pick("dk_sc_picked", d_sc[:], k1_l, U8)
+        dk_w_picked = pick("dk_w_picked", d_w[:].bitcast(U32), k1_l, U32)
+        dk_sc_dealt = deal("dk_sc_dealt", dk_sc_picked, U8)
+        dk_w = deal("dk_w", dk_w_picked, U32)
+        for q in range(4):
+            nc.sync.dma_start(
+                dk_sc[32 * q : 32 * q + 4, :].bitcast(I32),
+                dk_sc_dealt[32 * q : 32 * q + 32 : 8].rearrange("p t m -> p (t m)").bitcast(I32),
+            )
+
+        halves = [slice(0, HALF), slice(HALF, S)]
+        d_diff = [sb("d_diff%d" % t, [P, S], F32) for t in range(PACK)]
+        gate = sb("gate", [P, PACK, S], F32)
+        for t in range(PACK):
+            for cols in halves:
+                nc.vector.tensor_tensor(d_diff[t][:, cols], d_win[t][:].indirect(entries(n2_l, cols)), d_own[t][:, cols], ALU.subtract)
+            nc.scalar.activation(gate[:, t, :], d_diff[t][:], ACT.Sigmoid)
+
+        h_win = [sb("h_win%d" % t, [P, S], F32) for t in range(PACK)]
+        y_diff = sb("y_diff", [P, PACK, S], F32)
+        pull = sb("pull", [P, PACK, S], F32)
+        pieces = [slice(0, 256), slice(256, 384), slice(384, 512)]
+        for cols in halves:
+            for t in range(PACK):
+                nc.vector.tensor_tensor(y_diff[:, t, cols], y_win[t][:].indirect(entries(n1_l, cols)), y_own[:, t, cols], ALU.subtract)
+            mine = [(c, pc) for c, pc in enumerate(pieces) if cols.start <= pc.start < cols.stop]
+            for c, pc in mine:
+                nc.vector.tensor_tensor(pull[:, :, pc], y_diff[:, :, pc], gate[:, :, pc], ALU.mult)
+            z_bf = {}
+            for c, pc in mine:
+                width = pc.stop - pc.start
+                z_bf[c] = sb("z_bf%d" % c, [P, width, PACK], BF16)
+                nc.vector.tensor_tensor(
+                    z_bf[c][:].rearrange("p (c i) t -> p c t i", i=4),
+                    pull[:, :, pc].rearrange("p t (c i) -> p c t i", i=4),
+                    y_own[:, :, pc].rearrange("p t (c i) -> p c t i", i=4),
+                    ALU.add,
+                )
+            for c, pc in mine:
+                width = pc.stop - pc.start
+                z_w = sb("z_w%d" % c, [P, width], U32)
+                z_sc = sb("z_sc%d" % c, [P, width], U8)
+                nc.vector.quantize_mx(out=z_w[:].bitcast(FP8X4), scales=z_sc[:], in_=z_bf[c][:].rearrange("p c t -> p (c t)"))
+                for t in range(PACK):
+                    acc = banks[PACK * (c % 2) + t][:, 0:width]
+                    nc.tensor.matmul_mx(
+                        out=acc, lhsT=dk_w[:, t, :].bitcast(FP8X4), lhsT_scale=dk_sc[:, t * P : (t + 1) * P],
+                        rhs=z_w[:].bitcast(FP8X4), rhs_scale=z_sc[:], start=True, stop=True,
+                    )
+                    nc.scalar.activation(h_win[t][:, pc], acc, ACT.Copy, scale=0.0625)
+
+        out_rows = out_0.rearrange("(p t) s -> p t s", t=PACK)
+        out_words = out_1[0].rearrange("p n t -> p (n t)").bitcast(I32)
+        o_sc = sb("o_sc", [P, S], U8)
+        for c, pc in enumerate(pieces):
+            width = pc.stop - pc.start
+            first = sb("first%d" % c, [P, PACK, width], F32)
+            prod = sb("prod%d" % c, [P, PACK, width], F32)
+            for t in range(PACK):
+                nc.vector.tensor_copy(first[:, t, :], h_win[t][:].indirect(entries(n3_l, pc)))
+            for t in range(PACK):
+                nc.vector.tensor_tensor(prod[:, t, :], h_win[t][:].indirect(entries(n4_l, pc)), first[:, t, :], ALU.mult)
+            nc.sync.dma_start(out_rows[:, :, pc], prod[:])
+            o_bf = sb("o_bf%d" % c, [P, width, PACK], BF16)
+            rounder = nc.vector.tensor_copy if pc.stop == S else nc.scalar.copy
+            rounder(o_bf[:].rearrange("p (c i) t -> p c t i", i=4), prod[:].rearrange("p t (c i) -> p c t i", i=4))
+            o_w = sb("o_w%d" % c, [P, width], I32)
+            nc.vector.quantize_mx(out=o_w[:].bitcast(FP8X4), scales=o_sc[:, pc], in_=o_bf[:].rearrange("p c t -> p (c t)"))
+            nc.sync.dma_start(out_words[:, pc], o_w[:])
+        for q in range(4):
+            queue = nc.scalar if q % 2 else nc.sync
+            queue.dma_start(out_2[0, 4 * q : 4 * q + 4, :].bitcast(I32), o_sc[32 * q : 32 * q + 4, :].bitcast(I32))

@@ -1,6 +1,7 @@
 from contextlib import ExitStack
 
 import concourse.mybir as mybir
+from concourse.masks import make_identity
 
 F32 = mybir.dt.float32
 BF16 = mybir.dt.bfloat16
@@ -30,10 +31,11 @@ def tile_picked_twqpullbprod_none_po_kernel(
     nc = tc.nc
     with ExitStack() as ctx:
         keep = ctx.enter_context(tc.tile_pool(name="keep", bufs=1))
+        reused = ctx.enter_context(tc.tile_pool(name="reused", bufs=1))
         psum = ctx.enter_context(tc.psum_pool(name="psum", bufs=1))
 
-        def sb(name, shape, dtype):
-            return keep.tile(shape, dtype, name=name, align_bytes=64)
+        def sb(name, shape, dtype, tag=None):
+            return keep.tile(shape, dtype, name=name, tag=tag or name, align_bytes=64)
 
         def load_list(name, src):
             tile = sb(name, [P, S // 16], U16)
@@ -43,59 +45,66 @@ def tile_picked_twqpullbprod_none_po_kernel(
         def entries(lst, cols):
             return lst[:, cols.start // 16 : cols.stop // 16]
 
-        def load_scale_rows(queue, plane, src):
+        def load_scale_rows(queues, plane, src):
             for q in range(4):
-                queue.dma_start(plane[32 * q : 32 * q + 4, :].bitcast(I32), src[0, 4 * q : 4 * q + 4, :].bitcast(I32))
+                queues[q % len(queues)].dma_start(plane[32 * q : 32 * q + 4, :].bitcast(I32), src[0, 4 * q : 4 * q + 4, :].bitcast(I32))
 
         def zeroed(engine, name, width):
             plane = sb(name, [P, width], U8)
             engine.memset(plane[:].bitcast(I32), 0)
             return plane
 
+        x_sc = zeroed(nc.gpsimd, "x_sc", T)
+        w2_sc_raw = zeroed(nc.gpsimd, "w2_sc_raw", K)
+        w1_sc_raw = zeroed(nc.gpsimd, "w1_sc_raw", K)
+        d_sc = zeroed(nc.vector, "d_sc", G)
+        dk_sc = zeroed(nc.vector, "dk_sc", K)
         warm = sb("warm", [P, 2], F32)
         nc.vector.memset(warm[:, 0:1], 0.0)
         nc.scalar.activation(warm[:, 1:2], warm[:, 0:1], ACT.Sigmoid)
+        d_win = [sb("d_win%d" % t, [P, 2 * S], F32) for t in range(PACK - 1)]
+        d_win.append(reused.tile([P, 2 * S], F32, name="d_win3", align_bytes=64, offset=0))
+        nc.gpsimd.memset(d_win[0][:, S:], 0.0)
+        ident = sb("ident", [P, P], F32)
+        make_identity(nc, ident[:])
 
-        w2_sc_raw = zeroed(nc.vector, "w2_sc_raw", K)
-        x_sc = zeroed(nc.vector, "x_sc", T)
-        w1_sc_raw = zeroed(nc.vector, "w1_sc_raw", K)
-        d_sc = zeroed(nc.gpsimd, "d_sc", G)
-        dk_sc = zeroed(nc.gpsimd, "dk_sc", K)
-
-        x_w = sb("x_w", [P, T], I32)
-        nc.sync.dma_start(x_w[:], x_words[0].rearrange("p n t -> p (n t)").bitcast(I32))
         two_l = load_list("two_l", two)
+        load_scale_rows([nc.sync], x_sc, x_scales)
         w2_raw = sb("w2_raw", [P, 2 * K], U8)
         nc.sync.dma_start(w2_raw[:].bitcast(I32), w2_words[0].bitcast(I32))
+        x_w = sb("x_w", [P, T], I32)
+        nc.sync.dma_start(x_w[:], x_words[0].rearrange("p n t -> p (n t)").bitcast(I32))
+        offs_l = load_list("offs_l", offs)
+        load_scale_rows([nc.sync], w2_sc_raw, w2_scales)
+        n2_l = load_list("n2_l", n2)
         w1_raw = sb("w1_raw", [P, 2 * K], U8)
         nc.sync.dma_start(w1_raw[:].bitcast(I32), w1_words[0].bitcast(I32))
-        load_scale_rows(nc.scalar, w2_sc_raw, w2_scales)
-        load_scale_rows(nc.sync, x_sc, x_scales)
-        offs_l = load_list("offs_l", offs)
-        load_scale_rows(nc.scalar, w1_sc_raw, w1_scales)
-        n2_l = load_list("n2_l", n2)
+        load_scale_rows([nc.sync], w1_sc_raw, w1_scales)
+        gs_sb = sb("gs_sb", [P, PACK], F32)
+        nc.sync.dma_start(gs_sb[:], gs.rearrange("(p t) o -> p (t o)", t=PACK))
         k1_l = load_list("k1_l", k1)
         d_w = sb("d_w", [P, G], I32)
         nc.sync.dma_start(d_w[:], d_words[0].rearrange("p n t -> p (n t)").bitcast(I32))
         nc.sync.dma_start(d_sc[0:P:8, :].bitcast(I32), d_scales[0].bitcast(I32))
-        gs_sb = sb("gs_sb", [P, PACK], F32)
-        nc.sync.dma_start(gs_sb[:], gs.rearrange("(p t) o -> p (t o)", t=PACK))
         n1_l = load_list("n1_l", n1)
         n3_l = load_list("n3_l", n3)
         n4_l = load_list("n4_l", n4)
 
         def deal_fp4(name, raw):
             dealt = sb(name, [P, PACK, P, 2], U8)
-            nc.vector.tensor_copy(dealt[:], raw[:].rearrange("p (m t b) -> p t m b", t=PACK, b=2))
+            nc.gpsimd.tensor_copy(dealt[:], raw[:].rearrange("p (m t b) -> p t m b", t=PACK, b=2))
             return dealt
 
-        def deal(name, raw, dtype):
+        def deal(engine, name, raw, dtype):
             dealt = sb(name, [P, PACK, P], dtype)
-            nc.vector.tensor_copy(dealt[:], raw[:].rearrange("p (m t) -> p t m", t=PACK))
+            engine.tensor_copy(dealt[:], raw[:].rearrange("p (m t) -> p t m", t=PACK))
             return dealt
 
-        def pick(name, window, lst, dtype):
-            picked = sb(name, [P, S], dtype)
+        def pick(name, window, lst, dtype, offset=None):
+            if offset is None:
+                picked = sb(name, [P, S], dtype)
+            else:
+                picked = reused.tile([P, S], dtype, name=name, align_bytes=64, offset=offset)
             nc.vector.tensor_copy(picked[:], window.indirect(lst[:]))
             return picked
 
@@ -110,96 +119,140 @@ def tile_picked_twqpullbprod_none_po_kernel(
                 )
 
         w2 = deal_fp4("w2", w2_raw)
+        w2_sc = deal(nc.gpsimd, "w2_sc", w2_sc_raw, U8)
         w1 = deal_fp4("w1", w1_raw)
-        w2_sc = deal("w2_sc", w2_sc_raw, U8)
-        x2_w = pick("x2_w", x_w[:].bitcast(U32), two_l, U32)
+        w1_sc = deal(nc.gpsimd, "w1_sc", w1_sc_raw, U8)
         x2_sc = pick("x2_sc", x_sc[:], two_l, U8)
+        x2_w = pick("x2_w", x_w[:].bitcast(U32), two_l, U32)
         project(0, w2, w2_sc, x2_w, x2_sc)
-        x1_w = pick("x1_w", x_w[:].bitcast(U32), offs_l, U32)
         x1_sc = pick("x1_sc", x_sc[:], offs_l, U8)
-        w1_sc = deal("w1_sc", w1_sc_raw, U8)
+        x1_w = pick("x1_w", x_w[:].bitcast(U32), offs_l, U32)
         project(PACK, w1, w1_sc, x1_w, x1_sc)
 
-        d_win = [sb("d_win%d" % t, [P, S], F32) for t in range(PACK)]
-        d_own = [sb("d_own%d" % t, [P, S], F32) for t in range(PACK)]
+        d_last = sb("d_last", [P, S], F32)
+        d_own = [d_win[t + 1][:, S:] for t in range(PACK - 1)] + [d_last[:]]
         for t in range(PACK):
-            nc.scalar.copy(d_win[t][:], banks[t][:])
-            nc.scalar.copy(d_own[t][:], banks[t][:])
-        y_win = [sb("y_win%d" % t, [P, S], F32) for t in range(PACK)]
-        y_own = sb("y_own", [P, PACK, S], F32)
-        for t in range(PACK):
-            nc.scalar.activation(y_win[t][:], banks[PACK + t][:], ACT.Copy, scale=gs_sb[:, t : t + 1])
-            nc.scalar.activation(y_own[:, t, :], banks[PACK + t][:], ACT.Copy, scale=gs_sb[:, t : t + 1])
+            nc.scalar.copy(d_win[t][:, :S], banks[t][:])
+            nc.scalar.copy(d_own[t], banks[t][:])
 
-        dk_sc_picked = pick("dk_sc_picked", d_sc[:], k1_l, U8)
-        dk_w_picked = pick("dk_w_picked", d_w[:].bitcast(U32), k1_l, U32)
-        dk_sc_dealt = deal("dk_sc_dealt", dk_sc_picked, U8)
-        dk_w = deal("dk_w", dk_w_picked, U32)
+        y_win = [sb("y_win%d" % t, [P, 2 * S], F32) for t in range(PACK)]
+        d_diff = [y_win[t][:, S:] for t in range(PACK)]
+        for t in range(PACK):
+            nc.vector.tensor_tensor(d_diff[t], d_win[t][:].indirect(n2_l[:]), d_own[t], ALU.subtract)
+
+        halves = [slice(0, HALF), slice(HALF, S)]
+        last = PACK - 1
+        gate_tiles = [sb("gate%d" % t, [P, S], F32) for t in range(last)]
+        gate_last = [sb("gate_last%d" % c, [P, HALF], F32) for c in range(2)]
+        gate = [[gate_tiles[t][:, cols] for cols in halves] for t in range(last)] + [[g[:] for g in gate_last]]
+        rest = [sb("rest%d" % t, [P, S], F32) for t in range(PACK)]
+
+        def scaled_y(t):
+            nc.scalar.activation(y_win[t][:, :S], banks[PACK + t][:], ACT.Copy, scale=gs_sb[:, t : t + 1])
+
+        def sigmoid(out, in_, sign):
+            nc.scalar.activation(out, in_, ACT.Sigmoid, scale=sign)
+
+        for t in (0, 1):
+            scaled_y(t)
+            sigmoid(rest[t][:], d_diff[t], -1.0)
+        for t in (0, 1):
+            sigmoid(gate_tiles[t][:], d_diff[t], 1.0)
+        scaled_y(2)
+        sigmoid(gate_tiles[2][:], d_diff[2], 1.0)
+        sigmoid(rest[2][:], d_diff[2], -1.0)
+        scaled_y(3)
+        sigmoid(rest[3][:], d_diff[3], -1.0)
+        for c, cols in enumerate(halves):
+            sigmoid(gate_last[c][:], d_diff[3][:, cols], 1.0)
+
+        dk_sc_picked = pick("dk_sc_picked", d_sc[:], k1_l, U8, 4 * S)
+        dk_w_picked = pick("dk_w_picked", d_w[:].bitcast(U32), k1_l, U32, 0)
+        dk_sc_dealt = deal(nc.vector, "dk_sc_dealt", dk_sc_picked, U8)
+        dk_w = deal(nc.vector, "dk_w", dk_w_picked, U32)
         for q in range(4):
             nc.sync.dma_start(
                 dk_sc[32 * q : 32 * q + 4, :].bitcast(I32),
                 dk_sc_dealt[32 * q : 32 * q + 32 : 8].rearrange("p t m -> p (t m)").bitcast(I32),
             )
 
-        halves = [slice(0, HALF), slice(HALF, S)]
-        d_diff = [sb("d_diff%d" % t, [P, S], F32) for t in range(PACK)]
-        gate = sb("gate", [P, PACK, S], F32)
+        stay = sb("stay", [P, PACK, S], F32, "d_last")
         for t in range(PACK):
-            for cols in halves:
-                nc.vector.tensor_tensor(d_diff[t][:, cols], d_win[t][:].indirect(entries(n2_l, cols)), d_own[t][:, cols], ALU.subtract)
-            nc.scalar.activation(gate[:, t, :], d_diff[t][:], ACT.Sigmoid)
+            engine = nc.gpsimd if t < 2 else nc.vector
+            engine.tensor_tensor(stay[:, t, :], rest[t][:], y_win[t][:, :S], ALU.mult)
+
+        def pulled(c, tag):
+            pull = sb("pull%d" % c, [P, PACK, HALF], F32, tag)
+            for t in range(PACK):
+                nc.vector.tensor_tensor(pull[:, t, :], y_win[t][:].indirect(entries(n1_l, halves[c])), gate[t][c], ALU.mult)
+            return pull
+
+        z_bf = [sb("z_bf%d" % c, [P, HALF, PACK], BF16) for c in range(2)]
+        pull = pulled(0, None)
+        for t in range(PACK):
+            for b in range(2):
+                cols = slice(b * P, (b + 1) * P)
+                total = banks[b][:, t * P : (t + 1) * P]
+                nc.tensor.matmul(total, stay[:, t, cols], ident[:], start=True, stop=False, is_transpose=True)
+                nc.tensor.matmul(total, pull[:, t, cols], ident[:], start=False, stop=True, is_transpose=True)
+        for b in range(2):
+            turned = sb("turned%d" % b, [P, 2, P, 2], BF16)
+            nc.scalar.copy(turned[:], banks[b][:].rearrange("j (u e m) -> j u m e", u=2, e=2))
+            pairs = turned[:].rearrange("j u m e -> j u (m e)").bitcast(F32)
+            for u in range(2):
+                nc.tensor.transpose(banks[2 + b][:, u * P : (u + 1) * P], pairs[:, u, :], ident[:])
+        for b in range(2):
+            nc.scalar.copy(
+                z_bf[0][:, b * P : (b + 1) * P, :].bitcast(F32),
+                banks[2 + b][:, 0 : 2 * P].rearrange("p (u j) -> p j u", u=2),
+            )
+        pull = pulled(1, "gate_last0")
+        nc.vector.tensor_tensor(
+            z_bf[1][:].rearrange("p (c i) t -> p c t i", i=4),
+            pull[:].rearrange("p t (c i) -> p c t i", i=4),
+            stay[:, :, halves[1]].rearrange("p t (c i) -> p c t i", i=4),
+            ALU.add,
+        )
 
         h_win = [sb("h_win%d" % t, [P, S], F32) for t in range(PACK)]
-        y_diff = sb("y_diff", [P, PACK, S], F32)
-        pull = sb("pull", [P, PACK, S], F32)
         pieces = [slice(0, 256), slice(256, 384), slice(384, 512)]
-        for cols in halves:
-            for t in range(PACK):
-                nc.vector.tensor_tensor(y_diff[:, t, cols], y_win[t][:].indirect(entries(n1_l, cols)), y_own[:, t, cols], ALU.subtract)
-            mine = [(c, pc) for c, pc in enumerate(pieces) if cols.start <= pc.start < cols.stop]
-            for c, pc in mine:
-                nc.vector.tensor_tensor(pull[:, :, pc], y_diff[:, :, pc], gate[:, :, pc], ALU.mult)
-            z_bf = {}
-            for c, pc in mine:
-                width = pc.stop - pc.start
-                z_bf[c] = sb("z_bf%d" % c, [P, width, PACK], BF16)
-                nc.vector.tensor_tensor(
-                    z_bf[c][:].rearrange("p (c i) t -> p c t i", i=4),
-                    pull[:, :, pc].rearrange("p t (c i) -> p c t i", i=4),
-                    y_own[:, :, pc].rearrange("p t (c i) -> p c t i", i=4),
-                    ALU.add,
+        z_w, z_sc = [], []
+        for c in range(2):
+            z_w.append(sb("z_w%d" % c, [P, HALF], U32))
+            z_sc.append(sb("z_sc%d" % c, [P, HALF], U8))
+            nc.vector.quantize_mx(out=z_w[c][:].bitcast(FP8X4), scales=z_sc[c][:], in_=z_bf[c][:].rearrange("p c t -> p (c t)"))
+
+        for t in range(PACK):
+            for c, pc in enumerate(halves):
+                acc = banks[PACK * (1 - c) + t][:, 0:HALF]
+                nc.tensor.matmul_mx(
+                    out=acc, lhsT=dk_w[:, t, :].bitcast(FP8X4), lhsT_scale=dk_sc[:, t * P : (t + 1) * P],
+                    rhs=z_w[c][:].bitcast(FP8X4), rhs_scale=z_sc[c][:], start=True, stop=True,
                 )
-            for c, pc in mine:
-                width = pc.stop - pc.start
-                z_w = sb("z_w%d" % c, [P, width], U32)
-                z_sc = sb("z_sc%d" % c, [P, width], U8)
-                nc.vector.quantize_mx(out=z_w[:].bitcast(FP8X4), scales=z_sc[:], in_=z_bf[c][:].rearrange("p c t -> p (c t)"))
-                for t in range(PACK):
-                    acc = banks[PACK * (c % 2) + t][:, 0:width]
-                    nc.tensor.matmul_mx(
-                        out=acc, lhsT=dk_w[:, t, :].bitcast(FP8X4), lhsT_scale=dk_sc[:, t * P : (t + 1) * P],
-                        rhs=z_w[:].bitcast(FP8X4), rhs_scale=z_sc[:], start=True, stop=True,
-                    )
-                    nc.scalar.activation(h_win[t][:, pc], acc, ACT.Copy, scale=0.0625)
+                nc.scalar.activation(h_win[t][:, pc], acc, ACT.Copy, scale=0.0625)
 
         out_rows = out_0.rearrange("(p t) s -> p t s", t=PACK)
         out_words = out_1[0].rearrange("p n t -> p (n t)").bitcast(I32)
         o_sc = sb("o_sc", [P, S], U8)
-        for c, pc in enumerate(pieces):
-            width = pc.stop - pc.start
-            first = sb("first%d" % c, [P, PACK, width], F32)
-            prod = sb("prod%d" % c, [P, PACK, width], F32)
+        for g, cols in enumerate([slice(0, 384), slice(384, S)]):
+            first = sb("first%d" % g, [P, PACK, cols.stop - cols.start], F32)
+            prod = sb("prod%d" % g, [P, PACK, cols.stop - cols.start], F32)
             for t in range(PACK):
-                nc.vector.tensor_copy(first[:, t, :], h_win[t][:].indirect(entries(n3_l, pc)))
+                nc.vector.tensor_copy(first[:, t, :], h_win[t][:].indirect(entries(n3_l, cols)))
             for t in range(PACK):
-                nc.vector.tensor_tensor(prod[:, t, :], h_win[t][:].indirect(entries(n4_l, pc)), first[:, t, :], ALU.mult)
-            nc.sync.dma_start(out_rows[:, :, pc], prod[:])
-            o_bf = sb("o_bf%d" % c, [P, width, PACK], BF16)
-            rounder = nc.vector.tensor_copy if pc.stop == S else nc.scalar.copy
-            rounder(o_bf[:].rearrange("p (c i) t -> p c t i", i=4), prod[:].rearrange("p t (c i) -> p c t i", i=4))
-            o_w = sb("o_w%d" % c, [P, width], I32)
-            nc.vector.quantize_mx(out=o_w[:].bitcast(FP8X4), scales=o_sc[:, pc], in_=o_bf[:].rearrange("p c t -> p (c t)"))
-            nc.sync.dma_start(out_words[:, pc], o_w[:])
+                nc.vector.tensor_tensor(prod[:, t, :], h_win[t][:].indirect(entries(n4_l, cols)), first[:, t, :], ALU.mult)
+            nc.sync.dma_start(out_rows[:, :, cols], prod[:])
+            for c, pc in enumerate(pieces):
+                if not cols.start <= pc.start < cols.stop:
+                    continue
+                width = pc.stop - pc.start
+                here = slice(pc.start - cols.start, pc.stop - cols.start)
+                o_bf = sb("o_bf%d" % c, [P, width, PACK], BF16)
+                rounder = nc.vector.tensor_copy if pc.stop == S else nc.scalar.copy
+                rounder(o_bf[:].rearrange("p (c i) t -> p c t i", i=4), prod[:, :, here].rearrange("p t (c i) -> p c t i", i=4))
+                o_w = sb("o_w%d" % c, [P, width], I32)
+                nc.vector.quantize_mx(out=o_w[:].bitcast(FP8X4), scales=o_sc[:, pc], in_=o_bf[:].rearrange("p c t -> p (c t)"))
+                nc.sync.dma_start(out_words[:, pc], o_w[:])
         for q in range(4):
             queue = nc.scalar if q % 2 else nc.sync
             queue.dma_start(out_2[0, 4 * q : 4 * q + 4, :].bitcast(I32), o_sc[32 * q : 32 * q + 4, :].bitcast(I32))

@@ -110,13 +110,12 @@ def tile_picked_twqpullbprod_none_po_kernel(
 
         banks = [psum.tile([P, S], F32, name="bank%d" % b) for b in range(8)]
 
-        def project(first_bank, w, w_sc, xw, xs):
-            for t in range(PACK):
-                nc.tensor.matmul_mx(
-                    out=banks[first_bank + t][:],
-                    lhsT=w[:, t].rearrange("p m b -> p (m b)").bitcast(FP4X4), lhsT_scale=w_sc[:, t, :],
-                    rhs=xw[:].bitcast(FP8X4), rhs_scale=xs[:], start=True, stop=True,
-                )
+        def project(out, t, cols, w, w_sc, xw, xs):
+            nc.tensor.matmul_mx(
+                out=out,
+                lhsT=w[:, t].rearrange("p m b -> p (m b)").bitcast(FP4X4), lhsT_scale=w_sc[:, t, :],
+                rhs=xw[:, cols].bitcast(FP8X4), rhs_scale=xs[:, cols], start=True, stop=True,
+            )
 
         w2 = deal_fp4("w2", w2_raw)
         w2_sc = deal(nc.gpsimd, "w2_sc", w2_sc_raw, U8)
@@ -124,23 +123,27 @@ def tile_picked_twqpullbprod_none_po_kernel(
         w1_sc = deal(nc.gpsimd, "w1_sc", w1_sc_raw, U8)
         x2_sc = pick("x2_sc", x_sc[:], two_l, U8)
         x2_w = pick("x2_w", x_w[:].bitcast(U32), two_l, U32)
-        project(0, w2, w2_sc, x2_w, x2_sc)
+        halves = [slice(0, HALF), slice(HALF, S)]
+        d_parts = [(0, halves[0], banks[0][:, :HALF]), (0, halves[1], banks[2 * PACK - 1][:, :HALF])]
+        d_parts = d_parts + [(t, slice(0, S), banks[t][:]) for t in range(1, PACK)]
+        for t, cols, acc in d_parts:
+            project(acc, t, cols, w2, w2_sc, x2_w, x2_sc)
         x1_sc = pick("x1_sc", x_sc[:], offs_l, U8)
         x1_w = pick("x1_w", x_w[:].bitcast(U32), offs_l, U32)
-        project(PACK, w1, w1_sc, x1_w, x1_sc)
 
         d_last = sb("d_last", [P, S], F32)
         d_own = [d_win[t + 1][:, S:] for t in range(PACK - 1)] + [d_last[:]]
+        for t, cols, acc in d_parts:
+            nc.scalar.copy(d_win[t][:, cols], acc)
+            nc.scalar.copy(d_own[t][:, cols], acc)
         for t in range(PACK):
-            nc.scalar.copy(d_win[t][:, :S], banks[t][:])
-            nc.scalar.copy(d_own[t], banks[t][:])
+            project(banks[PACK + t][:], t, slice(0, S), w1, w1_sc, x1_w, x1_sc)
 
         y_win = [sb("y_win%d" % t, [P, 2 * S], F32) for t in range(PACK)]
         d_diff = [y_win[t][:, S:] for t in range(PACK)]
         for t in range(PACK):
             nc.vector.tensor_tensor(d_diff[t], d_win[t][:].indirect(n2_l[:]), d_own[t], ALU.subtract)
 
-        halves = [slice(0, HALF), slice(HALF, S)]
         last = PACK - 1
         gate_tiles = [sb("gate%d" % t, [P, S], F32) for t in range(last)]
         gate_last = [sb("gate_last%d" % c, [P, HALF], F32) for c in range(2)]
@@ -169,7 +172,8 @@ def tile_picked_twqpullbprod_none_po_kernel(
         dk_sc_picked = pick("dk_sc_picked", d_sc[:], k1_l, U8, 4 * S)
         dk_w_picked = pick("dk_w_picked", d_w[:].bitcast(U32), k1_l, U32, 0)
         dk_sc_dealt = deal(nc.vector, "dk_sc_dealt", dk_sc_picked, U8)
-        dk_w = deal(nc.vector, "dk_w", dk_w_picked, U32)
+        dk_first = sb("dk_first", [P, P], U32)
+        nc.vector.tensor_copy(dk_first[:], dk_w_picked[:, 0:S:PACK])
         for q in range(4):
             nc.sync.dma_start(
                 dk_sc[32 * q : 32 * q + 4, :].bitcast(I32),
@@ -187,7 +191,8 @@ def tile_picked_twqpullbprod_none_po_kernel(
                 nc.vector.tensor_tensor(pull[:, t, :], y_win[t][:].indirect(entries(n1_l, halves[c])), gate[t][c], ALU.mult)
             return pull
 
-        z_bf = [sb("z_bf%d" % c, [P, HALF, PACK], BF16) for c in range(2)]
+        pieces = [slice(0, 256), slice(256, 384), slice(384, 512)]
+        z_bf = [sb("z_bf%d" % c, [P, pc.stop - pc.start, PACK], BF16) for c, pc in enumerate(pieces)]
         pull = pulled(0, None)
         for t in range(PACK):
             for b in range(2):
@@ -207,29 +212,33 @@ def tile_picked_twqpullbprod_none_po_kernel(
                 banks[2 + b][:, 0 : 2 * P].rearrange("p (u j) -> p j u", u=2),
             )
         pull = pulled(1, "gate_last0")
-        nc.vector.tensor_tensor(
-            z_bf[1][:].rearrange("p (c i) t -> p c t i", i=4),
-            pull[:].rearrange("p t (c i) -> p c t i", i=4),
-            stay[:, :, halves[1]].rearrange("p t (c i) -> p c t i", i=4),
-            ALU.add,
-        )
+        for c in (1, 2):
+            pc = pieces[c]
+            nc.vector.tensor_tensor(
+                z_bf[c][:].rearrange("p (c i) t -> p c t i", i=4),
+                pull[:, :, pc.start - HALF : pc.stop - HALF].rearrange("p t (c i) -> p c t i", i=4),
+                stay[:, :, pc].rearrange("p t (c i) -> p c t i", i=4),
+                ALU.add,
+            )
 
         h_win = [sb("h_win%d" % t, [P, S], F32) for t in range(PACK)]
-        pieces = [slice(0, 256), slice(256, 384), slice(384, 512)]
         z_w, z_sc = [], []
-        for c in range(2):
-            z_w.append(sb("z_w%d" % c, [P, HALF], U32))
-            z_sc.append(sb("z_sc%d" % c, [P, HALF], U8))
+        for c, pc in enumerate(pieces):
+            z_w.append(sb("z_w%d" % c, [P, pc.stop - pc.start], U32))
+            z_sc.append(sb("z_sc%d" % c, [P, pc.stop - pc.start], U8, "z_bf0" if c == 1 else None))
             nc.vector.quantize_mx(out=z_w[c][:].bitcast(FP8X4), scales=z_sc[c][:], in_=z_bf[c][:].rearrange("p c t -> p (c t)"))
 
+        dk_rest = sb("dk_rest", [P, PACK - 1, P], U32, "z_bf2")
+        nc.vector.tensor_copy(dk_rest[:], dk_w_picked[:].rearrange("p (m t) -> p t m", t=PACK)[:, 1:, :])
+        dk_w = [dk_first[:]] + [dk_rest[:, t, :] for t in range(PACK - 1)]
         for t in range(PACK):
-            for c, pc in enumerate(halves):
-                acc = banks[PACK * (1 - c) + t][:, 0:HALF]
+            accs = [banks[PACK + t][:, 0:HALF], banks[t][:, 0:P], banks[(t + 2) % PACK][:, P : 2 * P]]
+            for c, pc in enumerate(pieces):
                 nc.tensor.matmul_mx(
-                    out=acc, lhsT=dk_w[:, t, :].bitcast(FP8X4), lhsT_scale=dk_sc[:, t * P : (t + 1) * P],
+                    out=accs[c], lhsT=dk_w[t].bitcast(FP8X4), lhsT_scale=dk_sc[:, t * P : (t + 1) * P],
                     rhs=z_w[c][:].bitcast(FP8X4), rhs_scale=z_sc[c][:], start=True, stop=True,
                 )
-                nc.scalar.activation(h_win[t][:, pc], acc, ACT.Copy, scale=0.0625)
+                nc.scalar.activation(h_win[t][:, pc], accs[c], ACT.Copy, scale=0.0625)
 
         out_rows = out_0.rearrange("(p t) s -> p t s", t=PACK)
         out_words = out_1[0].rearrange("p n t -> p (n t)").bitcast(I32)

from contextlib import ExitStack

import concourse.mybir as mybir
from concourse.masks import make_identity

F32 = mybir.dt.float32
BF16 = mybir.dt.bfloat16
I32 = mybir.dt.int32
U32 = mybir.dt.uint32
U16 = mybir.dt.uint16
U8 = mybir.dt.uint8
FP8X4 = mybir.dt.float8_e4m3fn_x4
FP4X4 = mybir.dt.float4_e2m1fn_x4
ACT = mybir.ActivationFunctionType
ALU = mybir.AluOpType

P = 128
PACK = 4
K = 512
T = 1024
S = 512
G = 2048
FLOPS = 3 * 2 * K * K * S
HALF = S // 2


def tile_picked_twqpullbprod_none_po_kernel(
    tc, x_words, x_scales, w1_words, w1_scales, w2_words, w2_scales, gs, d_words, d_scales,
    offs, two, n1, n2, k1, n3, n4, out_0, out_1, out_2,
):
    nc = tc.nc
    with ExitStack() as ctx:
        keep = ctx.enter_context(tc.tile_pool(name="keep", bufs=1))
        reused = ctx.enter_context(tc.tile_pool(name="reused", bufs=1))
        psum = ctx.enter_context(tc.psum_pool(name="psum", bufs=1))

        def sb(name, shape, dtype, tag=None):
            return keep.tile(shape, dtype, name=name, tag=tag or name, align_bytes=64)

        def load_list(name, src):
            tile = sb(name, [P, S // 16], U16)
            nc.sync.dma_start(tile[:], src)
            return tile

        def entries(lst, cols):
            return lst[:, cols.start // 16 : cols.stop // 16]

        def load_scale_rows(queues, plane, src):
            for q in range(4):
                queues[q % len(queues)].dma_start(plane[32 * q : 32 * q + 4, :].bitcast(I32), src[0, 4 * q : 4 * q + 4, :].bitcast(I32))

        def zeroed(engine, name, width):
            plane = sb(name, [P, width], U8)
            engine.memset(plane[:].bitcast(I32), 0)
            return plane

        x_sc = zeroed(nc.gpsimd, "x_sc", T)
        w2_sc_raw = zeroed(nc.gpsimd, "w2_sc_raw", K)
        w1_sc_raw = zeroed(nc.gpsimd, "w1_sc_raw", K)
        d_sc = zeroed(nc.vector, "d_sc", G)
        dk_sc = zeroed(nc.vector, "dk_sc", K)
        warm = sb("warm", [P, 2], F32)
        nc.vector.memset(warm[:, 0:1], 0.0)
        nc.scalar.activation(warm[:, 1:2], warm[:, 0:1], ACT.Sigmoid)
        d_win = [sb("d_win%d" % t, [P, 2 * S], F32) for t in range(PACK - 1)]
        d_win.append(reused.tile([P, 2 * S], F32, name="d_win3", align_bytes=64, offset=0))
        nc.gpsimd.memset(d_win[0][:, S:], 0.0)
        ident = sb("ident", [P, P], F32)
        make_identity(nc, ident[:])

        two_l = load_list("two_l", two)
        load_scale_rows([nc.sync], x_sc, x_scales)
        w2_raw = sb("w2_raw", [P, 2 * K], U8)
        nc.sync.dma_start(w2_raw[:].bitcast(I32), w2_words[0].bitcast(I32))
        x_w = sb("x_w", [P, T], I32)
        nc.sync.dma_start(x_w[:], x_words[0].rearrange("p n t -> p (n t)").bitcast(I32))
        offs_l = load_list("offs_l", offs)
        load_scale_rows([nc.sync], w2_sc_raw, w2_scales)
        n2_l = load_list("n2_l", n2)
        w1_raw = sb("w1_raw", [P, 2 * K], U8)
        nc.sync.dma_start(w1_raw[:].bitcast(I32), w1_words[0].bitcast(I32))
        load_scale_rows([nc.sync], w1_sc_raw, w1_scales)
        gs_sb = sb("gs_sb", [P, PACK], F32)
        nc.sync.dma_start(gs_sb[:], gs.rearrange("(p t) o -> p (t o)", t=PACK))
        k1_l = load_list("k1_l", k1)
        d_w = sb("d_w", [P, G], I32)
        nc.sync.dma_start(d_w[:], d_words[0].rearrange("p n t -> p (n t)").bitcast(I32))
        nc.sync.dma_start(d_sc[0:P:8, :].bitcast(I32), d_scales[0].bitcast(I32))
        n1_l = load_list("n1_l", n1)
        n3_l = load_list("n3_l", n3)
        n4_l = load_list("n4_l", n4)

        def deal_fp4(name, raw):
            dealt = sb(name, [P, PACK, P, 2], U8)
            nc.gpsimd.tensor_copy(dealt[:], raw[:].rearrange("p (m t b) -> p t m b", t=PACK, b=2))
            return dealt

        def deal(engine, name, raw, dtype):
            dealt = sb(name, [P, PACK, P], dtype)
            engine.tensor_copy(dealt[:], raw[:].rearrange("p (m t) -> p t m", t=PACK))
            return dealt

        def pick(name, window, lst, dtype, offset=None):
            if offset is None:
                picked = sb(name, [P, S], dtype)
            else:
                picked = reused.tile([P, S], dtype, name=name, align_bytes=64, offset=offset)
            nc.vector.tensor_copy(picked[:], window.indirect(lst[:]))
            return picked

        banks = [psum.tile([P, S], F32, name="bank%d" % b) for b in range(8)]

        def project(out, t, cols, w, w_sc, xw, xs):
            nc.tensor.matmul_mx(
                out=out,
                lhsT=w[:, t].rearrange("p m b -> p (m b)").bitcast(FP4X4), lhsT_scale=w_sc[:, t, :],
                rhs=xw[:, cols].bitcast(FP8X4), rhs_scale=xs[:, cols], start=True, stop=True,
            )

        w2 = deal_fp4("w2", w2_raw)
        w2_sc = deal(nc.gpsimd, "w2_sc", w2_sc_raw, U8)
        w1 = deal_fp4("w1", w1_raw)
        w1_sc = deal(nc.gpsimd, "w1_sc", w1_sc_raw, U8)
        x2_sc = pick("x2_sc", x_sc[:], two_l, U8)
        x2_w = pick("x2_w", x_w[:].bitcast(U32), two_l, U32)
        halves = [slice(0, HALF), slice(HALF, S)]
        d_parts = [(0, halves[0], banks[0][:, :HALF]), (0, halves[1], banks[2 * PACK - 1][:, :HALF])]
        d_parts = d_parts + [(t, slice(0, S), banks[t][:]) for t in range(1, PACK)]
        for t, cols, acc in d_parts:
            project(acc, t, cols, w2, w2_sc, x2_w, x2_sc)
        x1_sc = pick("x1_sc", x_sc[:], offs_l, U8)
        x1_w = pick("x1_w", x_w[:].bitcast(U32), offs_l, U32)

        d_last = sb("d_last", [P, S], F32)
        d_own = [d_win[t + 1][:, S:] for t in range(PACK - 1)] + [d_last[:]]
        for t, cols, acc in d_parts:
            nc.scalar.copy(d_win[t][:, cols], acc)
            nc.scalar.copy(d_own[t][:, cols], acc)
        for t in range(PACK):
            project(banks[PACK + t][:], t, slice(0, S), w1, w1_sc, x1_w, x1_sc)

        y_win = [sb("y_win%d" % t, [P, 2 * S], F32) for t in range(PACK)]
        d_diff = [y_win[t][:, S:] for t in range(PACK)]
        for t in range(PACK):
            nc.vector.tensor_tensor(d_diff[t], d_win[t][:].indirect(n2_l[:]), d_own[t], ALU.subtract)

        last = PACK - 1
        gate_tiles = [sb("gate%d" % t, [P, S], F32) for t in range(last)]
        gate_last = [sb("gate_last%d" % c, [P, HALF], F32) for c in range(2)]
        gate = [[gate_tiles[t][:, cols] for cols in halves] for t in range(last)] + [[g[:] for g in gate_last]]
        rest = [sb("rest%d" % t, [P, S], F32) for t in range(PACK)]

        def scaled_y(t):
            nc.scalar.activation(y_win[t][:, :S], banks[PACK + t][:], ACT.Copy, scale=gs_sb[:, t : t + 1])

        def sigmoid(out, in_, sign):
            nc.scalar.activation(out, in_, ACT.Sigmoid, scale=sign)

        for t in (0, 1):
            scaled_y(t)
            sigmoid(rest[t][:], d_diff[t], -1.0)
        for t in (0, 1):
            sigmoid(gate_tiles[t][:], d_diff[t], 1.0)
        scaled_y(2)
        sigmoid(gate_tiles[2][:], d_diff[2], 1.0)
        sigmoid(rest[2][:], d_diff[2], -1.0)
        scaled_y(3)
        sigmoid(rest[3][:], d_diff[3], -1.0)
        for c, cols in enumerate(halves):
            sigmoid(gate_last[c][:], d_diff[3][:, cols], 1.0)

        dk_sc_picked = pick("dk_sc_picked", d_sc[:], k1_l, U8, 4 * S)
        dk_w_picked = pick("dk_w_picked", d_w[:].bitcast(U32), k1_l, U32, 0)
        dk_sc_dealt = deal(nc.vector, "dk_sc_dealt", dk_sc_picked, U8)
        dk_first = sb("dk_first", [P, P], U32)
        nc.vector.tensor_copy(dk_first[:], dk_w_picked[:, 0:S:PACK])
        for q in range(4):
            nc.sync.dma_start(
                dk_sc[32 * q : 32 * q + 4, :].bitcast(I32),
                dk_sc_dealt[32 * q : 32 * q + 32 : 8].rearrange("p t m -> p (t m)").bitcast(I32),
            )

        stay = sb("stay", [P, PACK, S], F32, "d_last")
        for t in range(PACK):
            engine = nc.gpsimd if t < 2 else nc.vector
            engine.tensor_tensor(stay[:, t, :], rest[t][:], y_win[t][:, :S], ALU.mult)

        def pulled(c, tag):
            pull = sb("pull%d" % c, [P, PACK, HALF], F32, tag)
            for t in range(PACK):
                nc.vector.tensor_tensor(pull[:, t, :], y_win[t][:].indirect(entries(n1_l, halves[c])), gate[t][c], ALU.mult)
            return pull

        pieces = [slice(0, 256), slice(256, 384), slice(384, 512)]
        z_bf = [sb("z_bf%d" % c, [P, pc.stop - pc.start, PACK], BF16) for c, pc in enumerate(pieces)]
        pull = pulled(0, None)
        for t in range(PACK):
            for b in range(2):
                cols = slice(b * P, (b + 1) * P)
                total = banks[b][:, t * P : (t + 1) * P]
                nc.tensor.matmul(total, stay[:, t, cols], ident[:], start=True, stop=False, is_transpose=True)
                nc.tensor.matmul(total, pull[:, t, cols], ident[:], start=False, stop=True, is_transpose=True)
        for b in range(2):
            turned = sb("turned%d" % b, [P, 2, P, 2], BF16)
            nc.scalar.copy(turned[:], banks[b][:].rearrange("j (u e m) -> j u m e", u=2, e=2))
            pairs = turned[:].rearrange("j u m e -> j u (m e)").bitcast(F32)
            for u in range(2):
                nc.tensor.transpose(banks[2 + b][:, u * P : (u + 1) * P], pairs[:, u, :], ident[:])
        for b in range(2):
            nc.scalar.copy(
                z_bf[0][:, b * P : (b + 1) * P, :].bitcast(F32),
                banks[2 + b][:, 0 : 2 * P].rearrange("p (u j) -> p j u", u=2),
            )
        pull = pulled(1, "gate_last0")
        for c in (1, 2):
            pc = pieces[c]
            nc.vector.tensor_tensor(
                z_bf[c][:].rearrange("p (c i) t -> p c t i", i=4),
                pull[:, :, pc.start - HALF : pc.stop - HALF].rearrange("p t (c i) -> p c t i", i=4),
                stay[:, :, pc].rearrange("p t (c i) -> p c t i", i=4),
                ALU.add,
            )

        h_win = [sb("h_win%d" % t, [P, S], F32) for t in range(PACK)]
        z_w, z_sc = [], []
        for c, pc in enumerate(pieces):
            z_w.append(sb("z_w%d" % c, [P, pc.stop - pc.start], U32))
            z_sc.append(sb("z_sc%d" % c, [P, pc.stop - pc.start], U8, "z_bf0" if c == 1 else None))
            nc.vector.quantize_mx(out=z_w[c][:].bitcast(FP8X4), scales=z_sc[c][:], in_=z_bf[c][:].rearrange("p c t -> p (c t)"))

        dk_rest = sb("dk_rest", [P, PACK - 1, P], U32, "z_bf2")
        nc.vector.tensor_copy(dk_rest[:], dk_w_picked[:].rearrange("p (m t) -> p t m", t=PACK)[:, 1:, :])
        dk_w = [dk_first[:]] + [dk_rest[:, t, :] for t in range(PACK - 1)]
        for t in range(PACK):
            accs = [banks[PACK + t][:, 0:HALF], banks[t][:, 0:P], banks[(t + 2) % PACK][:, P : 2 * P]]
            for c, pc in enumerate(pieces):
                nc.tensor.matmul_mx(
                    out=accs[c], lhsT=dk_w[t].bitcast(FP8X4), lhsT_scale=dk_sc[:, t * P : (t + 1) * P],
                    rhs=z_w[c][:].bitcast(FP8X4), rhs_scale=z_sc[c][:], start=True, stop=True,
                )
                nc.scalar.activation(h_win[t][:, pc], accs[c], ACT.Copy, scale=0.0625)

        out_rows = out_0.rearrange("(p t) s -> p t s", t=PACK)
        out_words = out_1[0].rearrange("p n t -> p (n t)").bitcast(I32)
        o_sc = sb("o_sc", [P, S], U8)
        for g, cols in enumerate([slice(0, 384), slice(384, S)]):
            first = sb("first%d" % g, [P, PACK, cols.stop - cols.start], F32)
            prod = sb("prod%d" % g, [P, PACK, cols.stop - cols.start], F32)
            for t in range(PACK):
                nc.vector.tensor_copy(first[:, t, :], h_win[t][:].indirect(entries(n3_l, cols)))
            for t in range(PACK):
                nc.vector.tensor_tensor(prod[:, t, :], h_win[t][:].indirect(entries(n4_l, cols)), first[:, t, :], ALU.mult)
            nc.sync.dma_start(out_rows[:, :, cols], prod[:])
            for c, pc in enumerate(pieces):
                if not cols.start <= pc.start < cols.stop:
                    continue
                width = pc.stop - pc.start
                here = slice(pc.start - cols.start, pc.stop - cols.start)
                o_bf = sb("o_bf%d" % c, [P, width, PACK], BF16)
                rounder = nc.vector.tensor_copy if pc.stop == S else nc.scalar.copy
                rounder(o_bf[:].rearrange("p (c i) t -> p c t i", i=4), prod[:, :, here].rearrange("p t (c i) -> p c t i", i=4))
                o_w = sb("o_w%d" % c, [P, width], I32)
                nc.vector.quantize_mx(out=o_w[:].bitcast(FP8X4), scales=o_sc[:, pc], in_=o_bf[:].rearrange("p c t -> p (c t)"))
                nc.sync.dma_start(out_words[:, pc], o_w[:])
        for q in range(4):
            queue = nc.scalar if q % 2 else nc.sync
            queue.dma_start(out_2[0, 4 * q : 4 * q + 4, :].bitcast(I32), o_sc[32 * q : 32 * q + 4, :].bitcast(I32))
